import numpy as np
import ml_dtypes


def mxq(x, axis, fmt="e4m3"):
    dtype, down = {"e4m3": (ml_dtypes.float8_e4m3fn, 7), "e5m2": (ml_dtypes.float8_e5m2, 14)}[fmt]
    v = np.moveaxis(np.asarray(x, np.float32).astype(ml_dtypes.bfloat16).astype(np.float64), axis, -1)
    blocks = v.reshape(v.shape[:-1] + (-1, 32))
    amax = np.abs(blocks).max(-1, keepdims=True)
    byte = np.maximum(np.where(amax > 0, np.frexp(amax)[1] - 1 + 127, 0) - down, 1)
    scale = np.exp2(byte - 127.0)
    codes = (blocks / scale).astype(np.float32).astype(dtype).astype(np.float64)
    return np.moveaxis((codes * scale).reshape(v.shape), -1, axis)


WIDE = False


def mx_kscale(k):
    if not WIDE:
        return np.ones(k)
    levels = np.array([10, -10, 5, -5, 0])
    if k % 512:
        return np.exp2(np.random.permutation(np.resize(levels, k // 32))).repeat(32)
    a = np.empty((k // 512, 16))
    for p in range(k // 512):
        a[p, :8] = np.random.permutation(np.resize(levels, 8))
        for g in range(8):
            far = levels[np.abs(levels - a[p, g]) >= 10]
            a[p, g + 8] = far[np.random.randint(len(far))]
    return np.exp2(a.ravel()).repeat(32)


def f64(x):
    return np.asarray(x).astype(np.float64)


def striped(idx):
    return np.tile(idx.reshape(-1, 16).T, (8, 1)).astype(np.uint16)


def unstriped(offs):
    return offs[:16].T.reshape(-1).astype(np.int64)


E2M1 = np.array([0.0, 0.5, 1.0, 1.5, 2.0, 3.0, 4.0, 6.0, -0.0, -0.5, -1.0, -1.5, -2.0, -3.0, -4.0, -6.0])


def pack_weight(w, fmt):
    k, n = w.shape
    w = f64(np.asarray(w, np.float32).astype(ml_dtypes.bfloat16)).reshape(k // 32, 32, n)
    amax = np.abs(w).max(1)
    if fmt == "e4m3":
        byte = np.frexp(amax)[1] - 1 + 127 - 7
    else:
        mant, ex = np.frexp(amax / 6.0)
        byte = np.where(mant > 0.5, ex, ex - 1) + 127
    byte = np.clip(np.where(amax > 0, byte, 1), 1, 254)
    scaled = (w * np.exp2(127.0 - byte)[:, None, :]).reshape(k, n).astype(np.float32)
    by_word = np.ascontiguousarray(scaled.reshape(k // 512, 128, 4, n).transpose(0, 1, 3, 2))
    if fmt == "e4m3":
        words = by_word.astype(ml_dtypes.float8_e4m3fn).view(np.uint8)
    else:
        c = by_word.astype(ml_dtypes.float4_e2m1fn).view(np.uint8) & 0xF
        words = (c[..., 0::2] | (c[..., 1::2] << 4)).reshape(k // 512, 128, 2 * n)
    return np.ascontiguousarray(words), np.ascontiguousarray(byte.astype(np.uint8).reshape(k // 512, 16, n))


def unpack_weight(words, scales, fmt):
    g, _, n = scales.shape
    words = np.ascontiguousarray(words).reshape(g, 128, n, -1)
    if fmt == "e4m3":
        vals = words.view(ml_dtypes.float8_e4m3fn).astype(np.float64)
    else:
        nib = np.empty((g, 128, n, 4), np.uint8)
        nib[..., 0::2] = words & 0xF
        nib[..., 1::2] = words >> 4
        vals = E2M1[nib]
    vals = vals * np.repeat(np.exp2(scales.astype(np.float64) - 127.0), 8, axis=1)[..., None]
    return vals.transpose(0, 1, 3, 2).reshape(g * 512, n)


def gelu(v):
    return 0.5 * v * (1.0 + np.tanh(np.sqrt(2.0 / np.pi) * (v + 0.044715 * v**3)))


def striped8(idx):
    return np.concatenate([v.reshape(-1, 16).T for v in idx]).astype(np.uint16)


def unstriped8(offs):
    return np.stack([offs[16 * g:16 * g + 16].T.reshape(-1) for g in range(8)]).astype(np.int64)


def runs(v, idx8):
    k = np.arange(v.shape[0])
    return v[k[:, None], idx8[k % 512 // 64]]


K, K2, H, N, T, S, T2 = 1024, 512, 1024, 512, 2048, 1024, 2048


def setup_inputs():
    n = np.random.standard_normal
    s = mx_kscale(K)[:, None]
    s2 = mx_kscale(K2)[:, None]
    u = mx_kscale(H)[:, None]
    tab_words, tab_scales = pack_weight(n((K, T)) * s, "e4m3")
    tab2_words, tab2_scales = pack_weight(n((K2, T)) * s2, "e4m3")
    w2_words, w2_scales = pack_weight(0.8 * n((K2, H)) / np.sqrt(K2) / s2, "e2m1")
    return {
        "tab_words": tab_words, "tab_scales": tab_scales,
        "tab2_words": tab2_words, "tab2_scales": tab2_scales,
        "offs": striped8(np.stack([np.random.permutation(T)[:S] for _ in range(8)])),
        "offs2": striped(np.random.permutation(T)[:S]),
        "offs3": striped(np.random.permutation(T2)[:S]),
        "w1": (0.8 * n((K, H)) / np.sqrt(K) / s).astype(np.float32),
        "w2_words": w2_words, "w2_scales": w2_scales,
        "gain": (np.exp(0.3 * n(H)) * u[:, 0]).astype(np.float32),
        "w3": (1.5 * n((H, N)) / np.sqrt(H) / u).astype(np.float32),
        "page1": n((N, T2)).astype(np.float32),
        "wgo": np.exp(0.3 * n((128, S))).astype(np.float32),
    }


def reference(tab_words, tab_scales, tab2_words, tab2_scales, offs, offs2, offs3,
              w1, w2_words, w2_scales, gain, w3, page1, wgo):
    v = runs(unpack_weight(tab_words, tab_scales, "e4m3"), unstriped8(offs))
    v2 = unpack_weight(tab2_words, tab2_scales, "e4m3")[:, unstriped(offs2)]
    w2 = unpack_weight(w2_words, w2_scales, "e2m1")
    rod = mxq(f64(w1), 0, "e4m3").T @ v
    batch = w2.T @ v2
    z = np.tanh(np.maximum(rod, batch) + rod * batch) * f64(gain)[:, None]
    y = mxq(f64(w3), 0, "e4m3").T @ mxq(z, 0, "e4m3")
    out = f64(page1).copy()
    out[:, unstriped(offs3)] = np.tile(f64(wgo), (N // 128, 1)) * y
    return out

@@ -1,0 +1,298 @@
+from contextlib import ExitStack
+
+import concourse.mybir as mybir
+from concourse.masks import make_identity
+
+K, K2, H, N, T, S, T2 = 1024, 512, 1024, 512, 2048, 1024, 2048
+FLOPS = 2 * (K * H * S + K2 * H * S + H * N * S)
+
+F32 = mybir.dt.float32
+BF16 = mybir.dt.bfloat16
+I32 = mybir.dt.int32
+U32 = mybir.dt.uint32
+U16 = mybir.dt.uint16
+U8 = mybir.dt.uint8
+FP8X4 = mybir.dt.float8_e4m3fn_x4
+FP4X4 = mybir.dt.float4_e2m1fn_x4
+ALU = mybir.AluOpType
+ACT = mybir.ActivationFunctionType
+
+P = 128
+PACK = 4
+PASS = P * PACK
+CHUNK = 256
+LIST_ROWS = 16
+VECTOR_GAIN_CHUNKS = 2
+
+
+def tile_list_rod_batch_bench_kernel(
+    tc, tab_words, tab_scales, tab2_words, tab2_scales, offs, offs2, offs3,
+    w1, w2_words, w2_scales, gain, w3, page1, wgo, out,
+):
+    nc = tc.nc
+    with ExitStack() as ctx:
+        keep = ctx.enter_context(tc.tile_pool(name="keep", bufs=1))
+        stage = ctx.enter_context(tc.tile_pool(name="stage", bufs=2))
+        work = ctx.enter_context(tc.tile_pool(name="work", bufs=3))
+        large = ctx.enter_context(tc.tile_pool(name="large", bufs=4))
+        psum = ctx.enter_context(tc.psum_pool(name="psum", bufs=2))
+        ring = ctx.enter_context(tc.psum_pool(name="ring", bufs=4))
+
+        def held(name, shape, dtype):
+            return keep.tile(shape, dtype, name=name, align_bytes=64)
+
+        rod_list = held("rod_list", [P, S // LIST_ROWS], U16)
+        batch_list = held("batch_list", [P, S // LIST_ROWS], U16)
+        place_list = held("place_list", [P, S // LIST_ROWS], U16)
+
+        rod_scale_table = held("rod_scale_table", [P, T], U8)
+        batch_scale_table = held("batch_scale_table", [P, T], U8)
+        w2_plane = held("w2_plane", [P, H], U8)
+        for cleared in (rod_scale_table, batch_scale_table, w2_plane):
+            nc.vector.memset(cleared[:].bitcast(I32), 0)
+
+        def load_weight(name, rows):
+            raw = large.tile([P, PACK, PASS], F32, name=name, tag="large", align_bytes=64)
+            nc.sync.dma_start(out=raw[:], in_=rows.rearrange("(p t) c -> p t c", t=PACK))
+            return raw
+
+        def load_table(name, words):
+            table = large.tile([P, T], U32, name=name, tag="large", align_bytes=64)
+            nc.sync.dma_start(
+                out=table[:].bitcast(I32), in_=words.rearrange("p t i -> p (t i)").bitcast(I32)
+            )
+            return table
+
+        def load_page(i):
+            page = large.tile([P, T2], F32, name="page_%d" % i, tag="large", align_bytes=64)
+            nc.sync.dma_start(out=page[:], in_=page1[i * P : (i + 1) * P, :])
+            return page
+
+        def w1_piece(a, h):
+            return w1[a * PASS : (a + 1) * PASS, h * PASS : (h + 1) * PASS]
+
+        nc.sync.dma_start(rod_list[:], offs)
+        nc.sync.dma_start(batch_list[:], offs2)
+        nc.sync.dma_start(place_list[:], offs3)
+        w2_codes = held("w2_codes", [P, 2 * H], U8)
+        nc.sync.dma_start(out=w2_codes[:].bitcast(I32), in_=w2_words[0].bitcast(I32))
+        rod_rows = tab_scales.bitcast(I32).rearrange("a (g e) t -> e g a t", e=2)
+        for e in range(2):
+            nc.sync.dma_start(out=rod_scale_table[e:P:8, :].bitcast(I32), in_=rod_rows[e])
+        w1_raw = {(0, 0): load_weight("w1_raw_00", w1_piece(0, 0))}
+        for d in range(4):
+            nc.sync.dma_start(
+                out=batch_scale_table[32 * d : 32 * d + 4, :].bitcast(I32),
+                in_=tab2_scales[0, 4 * d : 4 * d + 4, :].bitcast(I32),
+            )
+        w1_raw[1, 0] = load_weight("w1_raw_10", w1_piece(1, 0))
+        tables = [load_table("rod_table_%d" % a, tab_words[a]) for a in range(2)]
+        for d in range(4):
+            nc.gpsimd.dma_start(
+                out=w2_plane[32 * d : 32 * d + 4, :].bitcast(I32),
+                in_=w2_scales[0, 4 * d : 4 * d + 4, :].bitcast(I32),
+            )
+        gain_sb = held("gain_sb", [P, 2, PACK], F32)
+        nc.gpsimd.dma_start(out=gain_sb[:], in_=gain.rearrange("(h p t) -> p h t", h=2, t=PACK))
+
+        identity = held("identity", [P, P], F32)
+        make_identity(nc, identity[:])
+
+        rod_scale_picked = held("rod_scale_picked", [P, S], U8)
+        nc.vector.tensor_copy(rod_scale_picked[:], rod_scale_table[:].indirect(rod_list[:]))
+        rod_plane = held("rod_plane", [P, S], U8)
+        nc.vector.tensor_copy(rod_plane[:].bitcast(I32), rod_scale_picked[:].bitcast(I32))
+        for a in range(2):
+            for e in range(2):
+                nc.scalar.dma_start(
+                    out=rod_plane[8 * a + 2 + e : P : 32, :].bitcast(I32),
+                    in_=rod_scale_picked[16 + 8 * a + e : P : 32, :].bitcast(I32),
+                )
+        batch_plane = held("batch_plane", [P, S], U8)
+        nc.vector.tensor_copy(batch_plane[:], batch_scale_table[:].indirect(batch_list[:]))
+
+        def quantize_weight(name, raw):
+            grouped = stage.tile([P, PASS, PACK], BF16, name="grouped", tag="grouped", align_bytes=64)
+            nc.scalar.copy(
+                out=grouped[:].rearrange("p (c i) t -> p c t i", i=4),
+                in_=raw[:].rearrange("p t (c i) -> p c t i", i=4),
+            )
+            codes = held(name + "_codes", [P, PASS], U32)
+            plane = held(name + "_plane", [P, PASS], U8)
+            nc.vector.quantize_mx(
+                out=codes[:].bitcast(FP8X4),
+                scales=plane[:],
+                in_=grouped[:].rearrange("p c t -> p (c t)"),
+            )
+            return codes, plane
+
+        w1_mx = {(a, 0): quantize_weight("w1_%d0" % a, w1_raw[a, 0]) for a in range(2)}
+
+        def pick_words(name, table, offsets):
+            words = held(name, [P, S], U32)
+            for lo, hi in ((0, CHUNK), (CHUNK, S)):
+                nc.vector.tensor_copy(
+                    words[:, lo:hi], table[:].indirect(offsets[:, lo // LIST_ROWS : hi // LIST_ROWS])
+                )
+            return words
+
+        batch_table = load_table("batch_table", tab2_words[0])
+        w1_raw[0, 1] = load_weight("w1_raw_01", w1_piece(0, 1))
+        picked = [pick_words("rod_words_0", tables[0], rod_list)]
+        w1_raw[1, 1] = load_weight("w1_raw_11", w1_piece(1, 1))
+        picked.append(pick_words("rod_words_1", tables[1], rod_list))
+        w3_raw = [load_weight("w3_raw_0", w3[0:PASS, :])]
+        picked.append(pick_words("batch_words", batch_table, batch_list))
+        w3_raw.append(load_weight("w3_raw_1", w3[PASS : 2 * PASS, :]))
+        pages = []
+
+        z_codes = [held("z_codes_%d" % h, [P, S], U32) for h in range(2)]
+        z_plane = [held("z_plane_%d" % h, [P, S], U8) for h in range(2)]
+        w3_mx = []
+
+        def first_products(jt, h):
+            cols = slice(jt * P, (jt + 1) * P)
+            batch = psum.tile([P, PASS], F32, name="batch")
+            nc.tensor.matmul_mx(
+                out=batch[:],
+                lhsT=picked[2][:, cols].bitcast(FP8X4),
+                lhsT_scale=batch_plane[:, cols],
+                rhs=w2_codes[:, 2 * h * PASS : 2 * (h + 1) * PASS].bitcast(FP4X4),
+                rhs_scale=w2_plane[:, h * PASS : (h + 1) * PASS],
+                start=True,
+                stop=True,
+            )
+            rod = psum.tile([P, PASS], F32, name="rod")
+            for a in range(2):
+                codes, plane = w1_mx[a, h]
+                nc.tensor.matmul_mx(
+                    out=rod[:],
+                    lhsT=picked[a][:, cols].bitcast(FP8X4),
+                    lhsT_scale=rod_plane[8 * a : P, cols],
+                    rhs=codes[:].bitcast(FP8X4),
+                    rhs_scale=plane[:],
+                    start=(a == 0),
+                    stop=(a == 1),
+                )
+            batch_sb = work.tile([P, PACK, P], F32, name="batch_sb")
+            nc.scalar.copy(out=batch_sb[:], in_=batch[:].rearrange("j (m t) -> j t m", t=PACK))
+            rod_dealt = rod[:].rearrange("j (m t) -> j t m", t=PACK)
+            larger = work.tile([P, PACK, P], F32, name="larger")
+            nc.vector.tensor_tensor(larger[:], rod_dealt, batch_sb[:], ALU.max)
+            product = work.tile([P, PACK, P], F32, name="product")
+            nc.vector.tensor_tensor(product[:], rod_dealt, batch_sb[:], ALU.mult)
+            return larger, product
+
+        bent_tiles = {}
+
+        def bend(jt, h, larger, product):
+            summed = ring.tile([P, PACK, P], F32, name="summed", tag="ring")
+            for t in range(PACK):
+                for term, first in ((larger, True), (product, False)):
+                    nc.tensor.matmul(
+                        summed[:, t, :], term[:, t, :], identity[:],
+                        start=first, stop=not first, is_transpose=True,
+                    )
+            c, jj = divmod(jt, CHUNK // P)
+            if jj == 0:
+                bent_tiles[c, h] = stage.tile([P, PACK * CHUNK], F32, name="bent")
+            bent = bent_tiles[c, h]
+            if c < VECTOR_GAIN_CHUNKS:
+                nc.scalar.activation(
+                    bent[:].rearrange("p (j t) -> p j t", t=PACK)[:, jj * P : (jj + 1) * P, :],
+                    summed[:].rearrange("p t j -> p j t"),
+                    ACT.Tanh,
+                )
+            else:
+                nc.scalar.activation(
+                    bent[:].rearrange("p (t j) -> p t j", t=PACK)[:, :, jj * P : (jj + 1) * P],
+                    summed[:],
+                    ACT.Tanh,
+                )
+
+        z_tiles = {}
+
+        def apply_gain(c, h):
+            bent = bent_tiles[c, h]
+            z = stage.tile([P, CHUNK, PACK], BF16, name="z", align_bytes=64)
+            if c < VECTOR_GAIN_CHUNKS:
+                nc.vector.tensor_tensor(
+                    z[:],
+                    bent[:].rearrange("p (j t) -> p j t", t=PACK),
+                    gain_sb[:, h, :].unsqueeze(1).to_broadcast([P, CHUNK, PACK]),
+                    ALU.mult,
+                )
+            else:
+                z_rows = stage.tile([P, PACK, CHUNK], BF16, name="z_rows")
+                for t in range(PACK):
+                    nc.scalar.activation(
+                        z_rows[:, t, :],
+                        bent[:, t * CHUNK : (t + 1) * CHUNK],
+                        ACT.Copy,
+                        scale=gain_sb[:, h, t : t + 1],
+                    )
+                nc.scalar.copy(
+                    out=z[:].rearrange("p (c i) t -> p c t i", i=4),
+                    in_=z_rows[:].rearrange("p t (c i) -> p c t i", i=4),
+                )
+            z_tiles[c, h] = z
+
+        def quantize_z(c, h):
+            cols = slice(c * CHUNK, (c + 1) * CHUNK)
+            nc.vector.quantize_mx(
+                out=z_codes[h][:, cols].bitcast(FP8X4),
+                scales=z_plane[h][:, cols],
+                in_=z_tiles[c, h][:].rearrange("p j t -> p (j t)"),
+            )
+
+        def place(c, i):
+            cols = slice(c * CHUNK, (c + 1) * CHUNK)
+            rows = slice(i * P, (i + 1) * P)
+            y = ring.tile([P, CHUNK], F32, name="y", tag="ring")
+            for h in range(2):
+                codes, plane = w3_mx[h]
+                nc.tensor.matmul_mx(
+                    out=y[:],
+                    lhsT=codes[:, rows].bitcast(FP8X4),
+                    lhsT_scale=plane[:, rows],
+                    rhs=z_codes[h][:, cols].bitcast(FP8X4),
+                    rhs_scale=z_plane[h][:, cols],
+                    start=(h == 0),
+                    stop=(h == 1),
+                )
+            y_sb = work.tile([P, CHUNK], F32, name="y_sb")
+            nc.scalar.copy(out=y_sb[:], in_=y[:])
+            offsets = place_list[:, c * CHUNK // LIST_ROWS : (c + 1) * CHUNK // LIST_ROWS]
+            nc.vector.tensor_tensor(pages[i][:].indirect(offsets), y_sb[:], wgo_sb[:, cols], ALU.mult)
+            if c == S // CHUNK - 1 and i < 3 or (c, i) == (3, 3):
+                nc.sync.dma_start(out=out[rows, :], in_=pages[i][:])
+
+        units = [(jt, h) for h in range(2) for jt in range(4)]
+        units = units + [(2 * c + jj, h) for c in (2, 3) for h in range(2) for jj in range(2)]
+        early = [(c, i) for c in range(2) for i in range(4)]
+        late = [(2, 0), (2, 1), (2, 2), (3, 0), (3, 1), (3, 2), (2, 3), (3, 3)]
+        terms = {}
+        for step in range(len(units) + 3):
+            if step < len(units):
+                terms[step] = first_products(*units[step])
+            if step in (0, 1):
+                w1_mx[step, 1] = quantize_weight("w1_%d1" % step, w1_raw[step, 1])
+                pages.append(load_page(step))
+            if step == 5:
+                wgo_sb = stage.tile([P, S], F32, name="wgo_sb", tag="grouped", align_bytes=64)
+                nc.sync.dma_start(out=wgo_sb[:], in_=wgo)
+            if step in (4, 5):
+                w3_mx.append(quantize_weight("w3_%d" % (step - 4), w3_raw[step - 4]))
+                pages.append(load_page(step - 2))
+            if 0 <= step - 1 < len(units):
+                bend(*units[step - 1], *terms[step - 1])
+            if 0 <= step - 2 < len(units) and units[step - 2][0] % 2 == 1:
+                apply_gain(units[step - 2][0] // 2, units[step - 2][1])
+            if 0 <= step - 3 < len(units) and units[step - 3][0] % 2 == 1:
+                quantize_z(units[step - 3][0] // 2, units[step - 3][1])
+            if 8 <= step < 16:
+                place(*early[step - 8])
+            if step >= 16:
+                place(*late[step - 16])
+        for c, i in late[3:]:
+            place(c, i)

@@ -73,9 +73,6 @@ def tile_list_rod_batch_bench_kernel(
 
         nc.sync.dma_start(rod_list[:], offs)
         nc.sync.dma_start(batch_list[:], offs2)
-        nc.sync.dma_start(place_list[:], offs3)
-        w2_codes = held("w2_codes", [P, 2 * H], U8)
-        nc.sync.dma_start(out=w2_codes[:].bitcast(I32), in_=w2_words[0].bitcast(I32))
         rod_rows = tab_scales.bitcast(I32).rearrange("a (g e) t -> e g a t", e=2)
         for e in range(2):
             nc.sync.dma_start(out=rod_scale_table[e:P:8, :].bitcast(I32), in_=rod_rows[e])
@@ -85,16 +82,12 @@ def tile_list_rod_batch_bench_kernel(
                 out=batch_scale_table[32 * d : 32 * d + 4, :].bitcast(I32),
                 in_=tab2_scales[0, 4 * d : 4 * d + 4, :].bitcast(I32),
             )
-        w1_raw[1, 0] = load_weight("w1_raw_10", w1_piece(1, 0))
         tables = [load_table("rod_table_%d" % a, tab_words[a]) for a in range(2)]
         for d in range(4):
             nc.gpsimd.dma_start(
                 out=w2_plane[32 * d : 32 * d + 4, :].bitcast(I32),
                 in_=w2_scales[0, 4 * d : 4 * d + 4, :].bitcast(I32),
             )
-        gain_sb = held("gain_sb", [P, 2, PACK], F32)
-        nc.gpsimd.dma_start(out=gain_sb[:], in_=gain.rearrange("(h p t) -> p h t", h=2, t=PACK))
-
         identity = held("identity", [P, P], F32)
         make_identity(nc, identity[:])
 
@@ -104,19 +97,23 @@ def tile_list_rod_batch_bench_kernel(
         nc.vector.tensor_copy(rod_plane[:].bitcast(I32), rod_scale_picked[:].bitcast(I32))
         for a in range(2):
             for e in range(2):
-                nc.scalar.dma_start(
+                nc.sync.dma_start(
                     out=rod_plane[8 * a + 2 + e : P : 32, :].bitcast(I32),
                     in_=rod_scale_picked[16 + 8 * a + e : P : 32, :].bitcast(I32),
                 )
+        w1_raw[1, 0] = load_weight("w1_raw_10", w1_piece(1, 0))
+        w2_codes = held("w2_codes", [P, 2 * H], U8)
+        nc.sync.dma_start(out=w2_codes[:].bitcast(I32), in_=w2_words[0].bitcast(I32))
         batch_plane = held("batch_plane", [P, S], U8)
         nc.vector.tensor_copy(batch_plane[:], batch_scale_table[:].indirect(batch_list[:]))
 
         def quantize_weight(name, raw):
             grouped = stage.tile([P, PASS, PACK], BF16, name="grouped", tag="grouped", align_bytes=64)
-            nc.scalar.copy(
-                out=grouped[:].rearrange("p (c i) t -> p c t i", i=4),
-                in_=raw[:].rearrange("p t (c i) -> p c t i", i=4),
-            )
+            for lo in range(0, PASS, P):
+                nc.scalar.copy(
+                    out=grouped[:, lo : lo + P, :].rearrange("p (c i) t -> p c t i", i=4),
+                    in_=raw[:, :, lo : lo + P].rearrange("p t (c i) -> p c t i", i=4),
+                )
             codes = held(name + "_codes", [P, PASS], U32)
             plane = held(name + "_plane", [P, PASS], U8)
             nc.vector.quantize_mx(
@@ -137,10 +134,13 @@ def tile_list_rod_batch_bench_kernel(
             return words
 
         batch_table = load_table("batch_table", tab2_words[0])
-        w1_raw[0, 1] = load_weight("w1_raw_01", w1_piece(0, 1))
+        gain_sb = held("gain_sb", [P, 2, PACK], F32)
+        nc.sync.dma_start(out=gain_sb[:], in_=gain.rearrange("(h p t) -> p h t", h=2, t=PACK))
+        nc.sync.dma_start(place_list[:], offs3)
         picked = [pick_words("rod_words_0", tables[0], rod_list)]
-        w1_raw[1, 1] = load_weight("w1_raw_11", w1_piece(1, 1))
+        w1_raw[0, 1] = load_weight("w1_raw_01", w1_piece(0, 1))
         picked.append(pick_words("rod_words_1", tables[1], rod_list))
+        w1_raw[1, 1] = load_weight("w1_raw_11", w1_piece(1, 1))
         w3_raw = [load_weight("w3_raw_0", w3[0:PASS, :])]
         picked.append(pick_words("batch_words", batch_table, batch_list))
         w3_raw.append(load_weight("w3_raw_1", w3[PASS : 2 * PASS, :]))

@@ -22,7 +22,7 @@ PACK = 4
 PASS = P * PACK
 CHUNK = 256
 LIST_ROWS = 16
-VECTOR_GAIN_CHUNKS = 2
+TILES = S // P
 
 
 def tile_list_rod_batch_bench_kernel(
@@ -35,11 +35,17 @@ def tile_list_rod_batch_bench_kernel(
         stage = ctx.enter_context(tc.tile_pool(name="stage", bufs=2))
         work = ctx.enter_context(tc.tile_pool(name="work", bufs=3))
         large = ctx.enter_context(tc.tile_pool(name="large", bufs=4))
-        psum = ctx.enter_context(tc.psum_pool(name="psum", bufs=2))
-        ring = ctx.enter_context(tc.psum_pool(name="ring", bufs=4))
+        psum = ctx.enter_context(tc.psum_pool(name="psum", bufs=1))
 
         def held(name, shape, dtype):
             return keep.tile(shape, dtype, name=name, align_bytes=64)
+
+        banks = [psum.tile([P, PASS], F32, name="bank_%d" % i) for i in range(8)]
+        late_uses = []
+
+        def late_bank():
+            late_uses.append(banks[5 + len(late_uses) % 3])
+            return late_uses[-1]
 
         rod_list = held("rod_list", [P, S // LIST_ROWS], U16)
         batch_list = held("batch_list", [P, S // LIST_ROWS], U16)
@@ -49,7 +55,7 @@ def tile_list_rod_batch_bench_kernel(
         batch_scale_table = held("batch_scale_table", [P, T], U8)
         w2_plane = held("w2_plane", [P, H], U8)
         for cleared in (rod_scale_table, batch_scale_table, w2_plane):
-            nc.vector.memset(cleared[:].bitcast(I32), 0)
+            nc.gpsimd.memset(cleared[:].bitcast(I32), 0)
 
         def load_weight(name, rows):
             raw = large.tile([P, PACK, PASS], F32, name=name, tag="large", align_bytes=64)
@@ -68,26 +74,67 @@ def tile_list_rod_batch_bench_kernel(
             nc.sync.dma_start(out=page[:], in_=page1[i * P : (i + 1) * P, :])
             return page
 
+        def load_scale_rows(queue, plane, rows):
+            for d in range(4):
+                queue.dma_start(
+                    out=plane[32 * d : 32 * d + 4, :].bitcast(I32),
+                    in_=rows[4 * d : 4 * d + 4, :].bitcast(I32),
+                )
+
         def w1_piece(a, h):
             return w1[a * PASS : (a + 1) * PASS, h * PASS : (h + 1) * PASS]
+
+        def round_columns(grouped, raw, lo, hi, late=False):
+            if late:
+                nc.gpsimd.tensor_scalar(
+                    out=grouped[:, lo:hi, :],
+                    in0=raw[:, :, lo:hi].rearrange("p t c -> p c t"),
+                    scalar1=1.0, scalar2=0.0, op0=ALU.mult, op1=ALU.add,
+                )
+            else:
+                nc.scalar.copy(
+                    out=grouped[:, lo:hi, :].rearrange("p (c i) t -> p c t i", i=4),
+                    in_=raw[:, :, lo:hi].rearrange("p t (c i) -> p c t i", i=4),
+                )
+
+        def new_grouped():
+            return stage.tile([P, PASS, PACK], BF16, name="grouped", tag="grouped", align_bytes=64)
+
+        def quantize_weight(name, grouped):
+            codes = held(name + "_codes", [P, PASS], U32)
+            plane = held(name + "_plane", [P, PASS], U8)
+            nc.vector.quantize_mx(
+                out=codes[:].bitcast(FP8X4),
+                scales=plane[:],
+                in_=grouped[:].rearrange("p c t -> p (c t)"),
+            )
+            return codes, plane
+
+        def early_weight(name, raw):
+            grouped = new_grouped()
+            for lo in range(0, PASS, P):
+                round_columns(grouped, raw, lo, lo + P)
+            return quantize_weight(name, grouped)
+
+        def pick_words(name, table, offsets):
+            words = held(name, [P, S], U32)
+            for lo, hi in ((0, CHUNK), (CHUNK, S)):
+                nc.vector.tensor_copy(
+                    words[:, lo:hi], table[:].indirect(offsets[:, lo // LIST_ROWS : hi // LIST_ROWS])
+                )
+            return words
 
         nc.sync.dma_start(rod_list[:], offs)
         nc.sync.dma_start(batch_list[:], offs2)
         rod_rows = tab_scales.bitcast(I32).rearrange("a (g e) t -> e g a t", e=2)
         for e in range(2):
             nc.sync.dma_start(out=rod_scale_table[e:P:8, :].bitcast(I32), in_=rod_rows[e])
-        w1_raw = {(0, 0): load_weight("w1_raw_00", w1_piece(0, 0))}
-        for d in range(4):
-            nc.sync.dma_start(
-                out=batch_scale_table[32 * d : 32 * d + 4, :].bitcast(I32),
-                in_=tab2_scales[0, 4 * d : 4 * d + 4, :].bitcast(I32),
-            )
-        tables = [load_table("rod_table_%d" % a, tab_words[a]) for a in range(2)]
-        for d in range(4):
-            nc.gpsimd.dma_start(
-                out=w2_plane[32 * d : 32 * d + 4, :].bitcast(I32),
-                in_=w2_scales[0, 4 * d : 4 * d + 4, :].bitcast(I32),
-            )
+        raw_00 = load_weight("w1_raw_00", w1_piece(0, 0))
+        load_scale_rows(nc.sync, batch_scale_table, tab2_scales[0])
+        rod_table_0 = load_table("rod_table_0", tab_words[0])
+        rod_table_1 = load_table("rod_table_1", tab_words[1])
+        load_scale_rows(nc.gpsimd, w2_plane, w2_scales[0])
+
         identity = held("identity", [P, P], F32)
         make_identity(nc, identity[:])
 
@@ -101,58 +148,49 @@ def tile_list_rod_batch_bench_kernel(
                     out=rod_plane[8 * a + 2 + e : P : 32, :].bitcast(I32),
                     in_=rod_scale_picked[16 + 8 * a + e : P : 32, :].bitcast(I32),
                 )
-        w1_raw[1, 0] = load_weight("w1_raw_10", w1_piece(1, 0))
-        w2_codes = held("w2_codes", [P, 2 * H], U8)
-        nc.sync.dma_start(out=w2_codes[:].bitcast(I32), in_=w2_words[0].bitcast(I32))
+        raw_10 = large.tile([P, PACK, PASS], F32, name="w1_raw_10", tag="large", align_bytes=64)
+        for lo in (0, PASS // 2):
+            nc.sync.dma_start(
+                out=raw_10[:, :, lo : lo + PASS // 2],
+                in_=w1_piece(1, 0)[:, lo : lo + PASS // 2].rearrange("(p t) c -> p t c", t=PACK),
+            )
         batch_plane = held("batch_plane", [P, S], U8)
         nc.vector.tensor_copy(batch_plane[:], batch_scale_table[:].indirect(batch_list[:]))
 
-        def quantize_weight(name, raw):
-            grouped = stage.tile([P, PASS, PACK], BF16, name="grouped", tag="grouped", align_bytes=64)
-            for lo in range(0, PASS, P):
-                nc.scalar.copy(
-                    out=grouped[:, lo : lo + P, :].rearrange("p (c i) t -> p c t i", i=4),
-                    in_=raw[:, :, lo : lo + P].rearrange("p t (c i) -> p c t i", i=4),
-                )
-            codes = held(name + "_codes", [P, PASS], U32)
-            plane = held(name + "_plane", [P, PASS], U8)
-            nc.vector.quantize_mx(
-                out=codes[:].bitcast(FP8X4),
-                scales=plane[:],
-                in_=grouped[:].rearrange("p c t -> p (c t)"),
-            )
-            return codes, plane
-
-        w1_mx = {(a, 0): quantize_weight("w1_%d0" % a, w1_raw[a, 0]) for a in range(2)}
-
-        def pick_words(name, table, offsets):
-            words = held(name, [P, S], U32)
-            for lo, hi in ((0, CHUNK), (CHUNK, S)):
-                nc.vector.tensor_copy(
-                    words[:, lo:hi], table[:].indirect(offsets[:, lo // LIST_ROWS : hi // LIST_ROWS])
-                )
-            return words
-
+        w1_mx = {(0, 0): early_weight("w1_00", raw_00), (1, 0): early_weight("w1_10", raw_10)}
         batch_table = load_table("batch_table", tab2_words[0])
+        w2_codes = held("w2_codes", [P, 2 * H], U8)
+        nc.sync.dma_start(out=w2_codes[:].bitcast(I32), in_=w2_words[0].bitcast(I32))
         gain_sb = held("gain_sb", [P, 2, PACK], F32)
         nc.sync.dma_start(out=gain_sb[:], in_=gain.rearrange("(h p t) -> p h t", h=2, t=PACK))
         nc.sync.dma_start(place_list[:], offs3)
-        picked = [pick_words("rod_words_0", tables[0], rod_list)]
-        w1_raw[0, 1] = load_weight("w1_raw_01", w1_piece(0, 1))
-        picked.append(pick_words("rod_words_1", tables[1], rod_list))
-        w1_raw[1, 1] = load_weight("w1_raw_11", w1_piece(1, 1))
-        w3_raw = [load_weight("w3_raw_0", w3[0:PASS, :])]
+        picked = [pick_words("rod_words_0", rod_table_0, rod_list)]
+        late_raw = [load_weight("w1_raw_01", w1_piece(0, 1))]
+        picked.append(pick_words("rod_words_1", rod_table_1, rod_list))
+        late_raw.append(load_weight("w1_raw_11", w1_piece(1, 1)))
+        late_raw.append(load_weight("w3_raw_0", w3[0:PASS, :]))
         picked.append(pick_words("batch_words", batch_table, batch_list))
-        w3_raw.append(load_weight("w3_raw_1", w3[PASS : 2 * PASS, :]))
-        pages = []
+        late_raw.append(load_weight("w3_raw_1", w3[PASS : 2 * PASS, :]))
 
         z_codes = [held("z_codes_%d" % h, [P, S], U32) for h in range(2)]
         z_plane = [held("z_plane_%d" % h, [P, S], U8) for h in range(2)]
-        w3_mx = []
+        late_grouped = []
+        late_mx = []
+        pages = []
 
-        def first_products(jt, h):
+        def late_weight_half(step):
+            piece, half = divmod(step, 2)
+            if half == 0:
+                late_grouped.append(new_grouped())
+            for lo in range(half * 2 * P, (half + 1) * 2 * P, P):
+                round_columns(late_grouped[piece], late_raw[piece], lo, lo + P, True)
+            if half == 1:
+                pages.append(load_page(piece))
+
+        def first_products(step):
+            jt, h = units[step]
             cols = slice(jt * P, (jt + 1) * P)
-            batch = psum.tile([P, PASS], F32, name="batch")
+            batch = banks[step % 2]
             nc.tensor.matmul_mx(
                 out=batch[:],
                 lhsT=picked[2][:, cols].bitcast(FP8X4),
@@ -162,7 +200,7 @@ def tile_list_rod_batch_bench_kernel(
                 start=True,
                 stop=True,
             )
-            rod = psum.tile([P, PASS], F32, name="rod")
+            rod = banks[2 + step % 3]
             for a in range(2):
                 codes, plane = w1_mx[a, h]
                 nc.tensor.matmul_mx(
@@ -176,17 +214,24 @@ def tile_list_rod_batch_bench_kernel(
                 )
             batch_sb = work.tile([P, PACK, P], F32, name="batch_sb")
             nc.scalar.copy(out=batch_sb[:], in_=batch[:].rearrange("j (m t) -> j t m", t=PACK))
+            return rod, batch_sb
+
+        def combine(rod, batch_sb):
             rod_dealt = rod[:].rearrange("j (m t) -> j t m", t=PACK)
-            larger = work.tile([P, PACK, P], F32, name="larger")
+            larger = work.tile([P, PACK, P], F32, name="larger", bufs=16)
             nc.vector.tensor_tensor(larger[:], rod_dealt, batch_sb[:], ALU.max)
-            product = work.tile([P, PACK, P], F32, name="product")
+            product = work.tile([P, PACK, P], F32, name="product", bufs=16)
             nc.vector.tensor_tensor(product[:], rod_dealt, batch_sb[:], ALU.mult)
             return larger, product
 
+        def gain_on_vector(c, h):
+            return (c, h) == (0, 1)
+
         bent_tiles = {}
 
-        def bend(jt, h, larger, product):
-            summed = ring.tile([P, PACK, P], F32, name="summed", tag="ring")
+        def bend(step, larger, product):
+            jt, h = units[step]
+            summed = late_bank()[:].rearrange("p (t j) -> p t j", t=PACK)
             for t in range(PACK):
                 for term, first in ((larger, True), (product, False)):
                     nc.tensor.matmul(
@@ -197,16 +242,16 @@ def tile_list_rod_batch_bench_kernel(
             if jj == 0:
                 bent_tiles[c, h] = stage.tile([P, PACK * CHUNK], F32, name="bent")
             bent = bent_tiles[c, h]
-            if c < VECTOR_GAIN_CHUNKS:
+            if gain_on_vector(c, h):
                 nc.scalar.activation(
                     bent[:].rearrange("p (j t) -> p j t", t=PACK)[:, jj * P : (jj + 1) * P, :],
-                    summed[:].rearrange("p t j -> p j t"),
+                    summed.rearrange("p t j -> p j t"),
                     ACT.Tanh,
                 )
             else:
                 nc.scalar.activation(
                     bent[:].rearrange("p (t j) -> p t j", t=PACK)[:, :, jj * P : (jj + 1) * P],
-                    summed[:],
+                    summed,
                     ACT.Tanh,
                 )
 
@@ -215,7 +260,7 @@ def tile_list_rod_batch_bench_kernel(
         def apply_gain(c, h):
             bent = bent_tiles[c, h]
             z = stage.tile([P, CHUNK, PACK], BF16, name="z", align_bytes=64)
-            if c < VECTOR_GAIN_CHUNKS:
+            if gain_on_vector(c, h):
                 nc.vector.tensor_tensor(
                     z[:],
                     bent[:].rearrange("p (j t) -> p j t", t=PACK),
@@ -245,54 +290,62 @@ def tile_list_rod_batch_bench_kernel(
                 in_=z_tiles[c, h][:].rearrange("p j t -> p (j t)"),
             )
 
-        def place(c, i):
-            cols = slice(c * CHUNK, (c + 1) * CHUNK)
+        def place(lo, hi, i):
             rows = slice(i * P, (i + 1) * P)
-            y = ring.tile([P, CHUNK], F32, name="y", tag="ring")
+            y = late_bank()[:, 0 : hi - lo]
             for h in range(2):
-                codes, plane = w3_mx[h]
+                codes, plane = late_mx[2 + h]
                 nc.tensor.matmul_mx(
-                    out=y[:],
+                    out=y,
                     lhsT=codes[:, rows].bitcast(FP8X4),
                     lhsT_scale=plane[:, rows],
-                    rhs=z_codes[h][:, cols].bitcast(FP8X4),
-                    rhs_scale=z_plane[h][:, cols],
+                    rhs=z_codes[h][:, lo:hi].bitcast(FP8X4),
+                    rhs_scale=z_plane[h][:, lo:hi],
                     start=(h == 0),
                     stop=(h == 1),
                 )
-            y_sb = work.tile([P, CHUNK], F32, name="y_sb")
-            nc.scalar.copy(out=y_sb[:], in_=y[:])
-            offsets = place_list[:, c * CHUNK // LIST_ROWS : (c + 1) * CHUNK // LIST_ROWS]
-            nc.vector.tensor_tensor(pages[i][:].indirect(offsets), y_sb[:], wgo_sb[:, cols], ALU.mult)
-            if c == S // CHUNK - 1 and i < 3 or (c, i) == (3, 3):
+            y_sb = work.tile([P, hi - lo], F32, name="y_sb", bufs=4)
+            nc.scalar.copy(out=y_sb[:], in_=y)
+            offsets = place_list[:, lo // LIST_ROWS : hi // LIST_ROWS]
+            nc.vector.tensor_tensor(pages[i][:].indirect(offsets), y_sb[:], wgo_sb[:, lo:hi], ALU.mult)
+            if hi == S:
                 nc.sync.dma_start(out=out[rows, :], in_=pages[i][:])
 
-        units = [(jt, h) for h in range(2) for jt in range(4)]
-        units = units + [(2 * c + jj, h) for c in (2, 3) for h in range(2) for jj in range(2)]
-        early = [(c, i) for c in range(2) for i in range(4)]
-        late = [(2, 0), (2, 1), (2, 2), (3, 0), (3, 1), (3, 2), (2, 3), (3, 3)]
+        def place_chunk(c, i):
+            place(c * CHUNK, (c + 1) * CHUNK, i)
+
+        def finish_half(c, h, placed):
+            first = units.index((2 * c, h))
+            for step in (first, first + 1):
+                bend(step, *terms[step])
+            apply_gain(c, h)
+            quantize_z(c, h)
+            for c_placed, i in placed:
+                place_chunk(c_placed, i)
+
+        order = [(0, 0), (1, 0), (2, 0), (0, 1), (1, 1), (3, 0), (2, 1), (3, 1)]
+        units = [(2 * c + jj, h) for c, h in order for jj in range(2)]
+        steps = 2 * TILES
+        halves = {2: (0, 0), 5: (1, 0), 8: (0, 1), 10: (1, 1), 12: (2, 0), 14: (2, 1), 15: (3, 0), 16: (3, 1)}
+        ready = [(c, i) for c in range(3) for i in range(4)]
         terms = {}
-        for step in range(len(units) + 3):
-            if step < len(units):
-                terms[step] = first_products(*units[step])
-            if step in (0, 1):
-                w1_mx[step, 1] = quantize_weight("w1_%d1" % step, w1_raw[step, 1])
-                pages.append(load_page(step))
-            if step == 5:
+        sums = {0: first_products(0)}
+        for step in range(steps + 1):
+            if step + 1 < steps:
+                sums[step + 1] = first_products(step + 1)
+            if step < steps:
+                terms[step] = combine(*sums[step])
+            if step in (2, 4, 6, 8):
+                late_mx.append(quantize_weight("late_%d" % step, late_grouped[len(late_mx)]))
+            if len(late_mx) == 2:
+                w1_mx[0, 1], w1_mx[1, 1] = late_mx
+            if step == 6:
                 wgo_sb = stage.tile([P, S], F32, name="wgo_sb", tag="grouped", align_bytes=64)
                 nc.sync.dma_start(out=wgo_sb[:], in_=wgo)
-            if step in (4, 5):
-                w3_mx.append(quantize_weight("w3_%d" % (step - 4), w3_raw[step - 4]))
-                pages.append(load_page(step - 2))
-            if 0 <= step - 1 < len(units):
-                bend(*units[step - 1], *terms[step - 1])
-            if 0 <= step - 2 < len(units) and units[step - 2][0] % 2 == 1:
-                apply_gain(units[step - 2][0] // 2, units[step - 2][1])
-            if 0 <= step - 3 < len(units) and units[step - 3][0] % 2 == 1:
-                quantize_z(units[step - 3][0] // 2, units[step - 3][1])
-            if 8 <= step < 16:
-                place(*early[step - 8])
-            if step >= 16:
-                place(*late[step - 16])
-        for c, i in late[3:]:
-            place(c, i)
+            if step in (0, 1, 2, 3, 4, 5, 6, 7):
+                late_weight_half((0, 1, 2, 3, 4, 5, 6, 7).index(step))
+            if step in halves:
+                done = sorted(halves).index(step) - 3
+                finish_half(*halves[step], ready[2 * done : 2 * done + 2] if done >= 0 else [])
+        for c, i in ((2, 2), (3, 0), (3, 1), (3, 2), (2, 3), (3, 3)):
+            place_chunk(c, i)

@@ -84,18 +84,11 @@ def tile_list_rod_batch_bench_kernel(
         def w1_piece(a, h):
             return w1[a * PASS : (a + 1) * PASS, h * PASS : (h + 1) * PASS]
 
-        def round_columns(grouped, raw, lo, hi, late=False):
-            if late:
-                nc.gpsimd.tensor_scalar(
-                    out=grouped[:, lo:hi, :],
-                    in0=raw[:, :, lo:hi].rearrange("p t c -> p c t"),
-                    scalar1=1.0, scalar2=0.0, op0=ALU.mult, op1=ALU.add,
-                )
-            else:
-                nc.scalar.copy(
-                    out=grouped[:, lo:hi, :].rearrange("p (c i) t -> p c t i", i=4),
-                    in_=raw[:, :, lo:hi].rearrange("p t (c i) -> p c t i", i=4),
-                )
+        def round_columns(grouped, raw, lo, hi):
+            nc.scalar.copy(
+                out=grouped[:, lo:hi, :].rearrange("p (c i) t -> p c t i", i=4),
+                in_=raw[:, :, lo:hi].rearrange("p t (c i) -> p c t i", i=4),
+            )
 
         def new_grouped():
             return stage.tile([P, PASS, PACK], BF16, name="grouped", tag="grouped", align_bytes=64)
@@ -183,7 +176,7 @@ def tile_list_rod_batch_bench_kernel(
             if half == 0:
                 late_grouped.append(new_grouped())
             for lo in range(half * 2 * P, (half + 1) * 2 * P, P):
-                round_columns(late_grouped[piece], late_raw[piece], lo, lo + P, True)
+                round_columns(late_grouped[piece], late_raw[piece], lo, lo + P)
             if half == 1:
                 pages.append(load_page(piece))
 
@@ -225,7 +218,7 @@ def tile_list_rod_batch_bench_kernel(
             return larger, product
 
         def gain_on_vector(c, h):
-            return (c, h) == (0, 1)
+            return c == 0 or (c, h) == (1, 0)
 
         bent_tiles = {}
 
@@ -335,15 +328,15 @@ def tile_list_rod_batch_bench_kernel(
                 sums[step + 1] = first_products(step + 1)
             if step < steps:
                 terms[step] = combine(*sums[step])
-            if step in (2, 4, 6, 8):
+            if step in (2, 4, 8, 10):
                 late_mx.append(quantize_weight("late_%d" % step, late_grouped[len(late_mx)]))
             if len(late_mx) == 2:
                 w1_mx[0, 1], w1_mx[1, 1] = late_mx
-            if step == 6:
+            if step == 8:
                 wgo_sb = stage.tile([P, S], F32, name="wgo_sb", tag="grouped", align_bytes=64)
                 nc.sync.dma_start(out=wgo_sb[:], in_=wgo)
-            if step in (0, 1, 2, 3, 4, 5, 6, 7):
-                late_weight_half((0, 1, 2, 3, 4, 5, 6, 7).index(step))
+            if step in (0, 1, 2, 3, 6, 7, 8, 9):
+                late_weight_half((0, 1, 2, 3, 6, 7, 8, 9).index(step))
             if step in halves:
                 done = sorted(halves).index(step) - 3
                 finish_half(*halves[step], ready[2 * done : 2 * done + 2] if done >= 0 else [])

@@ -20,9 +20,17 @@ ACT = mybir.ActivationFunctionType
 P = 128
 PACK = 4
 PASS = P * PACK
-CHUNK = 256
 LIST_ROWS = 16
-TILES = S // P
+CHUNK = 2 * P
+CHUNKS = S // CHUNK
+ROW_TILES = N // P
+
+PRODUCT_ORDER = [(0, 0), (1, 0), (2, 0), (0, 1), (1, 1), (3, 0), (2, 1), (3, 1)]
+FINISH_ORDER = [(0, 0), (1, 0), (0, 1), (1, 1), (2, 0), (2, 1), (3, 0), (3, 1)]
+FIRST_FINISH_STEP = 4
+W3_FIRST_STEP = 6
+VECTOR_GAIN_PARTS = 3
+BATCH_BANKS, ROD_BANKS, LATE_BANKS = 2, 3, 3
 
 
 def tile_list_rod_batch_bench_kernel(
@@ -34,22 +42,28 @@ def tile_list_rod_batch_bench_kernel(
         keep = ctx.enter_context(tc.tile_pool(name="keep", bufs=1))
         stage = ctx.enter_context(tc.tile_pool(name="stage", bufs=2))
         work = ctx.enter_context(tc.tile_pool(name="work", bufs=3))
-        large = ctx.enter_context(tc.tile_pool(name="large", bufs=4))
+        large = ctx.enter_context(tc.tile_pool(name="large", bufs=ROW_TILES))
         psum = ctx.enter_context(tc.psum_pool(name="psum", bufs=1))
 
         def held(name, shape, dtype):
             return keep.tile(shape, dtype, name=name, align_bytes=64)
 
+        def large_tile(name, shape, dtype):
+            return large.tile(shape, dtype, name=name, tag="large", align_bytes=64)
+
         banks = [psum.tile([P, PASS], F32, name="bank_%d" % i) for i in range(8)]
         late_uses = []
 
         def late_bank():
-            late_uses.append(banks[5 + len(late_uses) % 3])
+            late_uses.append(banks[BATCH_BANKS + ROD_BANKS + len(late_uses) % LATE_BANKS])
             return late_uses[-1]
 
         rod_list = held("rod_list", [P, S // LIST_ROWS], U16)
         batch_list = held("batch_list", [P, S // LIST_ROWS], U16)
         place_list = held("place_list", [P, S // LIST_ROWS], U16)
+
+        def entries(list_tile, lo, hi):
+            return list_tile[:, lo // LIST_ROWS : hi // LIST_ROWS]
 
         rod_scale_table = held("rod_scale_table", [P, T], U8)
         batch_scale_table = held("batch_scale_table", [P, T], U8)
@@ -57,20 +71,23 @@ def tile_list_rod_batch_bench_kernel(
         for cleared in (rod_scale_table, batch_scale_table, w2_plane):
             nc.gpsimd.memset(cleared[:].bitcast(I32), 0)
 
+        def by_partition(rows):
+            return rows.rearrange("(p t) c -> p t c", t=PACK)
+
         def load_weight(name, rows):
-            raw = large.tile([P, PACK, PASS], F32, name=name, tag="large", align_bytes=64)
-            nc.sync.dma_start(out=raw[:], in_=rows.rearrange("(p t) c -> p t c", t=PACK))
+            raw = large_tile(name, [P, PACK, PASS], F32)
+            nc.sync.dma_start(out=raw[:], in_=by_partition(rows))
             return raw
 
         def load_table(name, words):
-            table = large.tile([P, T], U32, name=name, tag="large", align_bytes=64)
+            table = large_tile(name, [P, T], U32)
             nc.sync.dma_start(
                 out=table[:].bitcast(I32), in_=words.rearrange("p t i -> p (t i)").bitcast(I32)
             )
             return table
 
         def load_page(i):
-            page = large.tile([P, T2], F32, name="page_%d" % i, tag="large", align_bytes=64)
+            page = large_tile("page_%d" % i, [P, T2], F32)
             nc.sync.dma_start(out=page[:], in_=page1[i * P : (i + 1) * P, :])
             return page
 
@@ -84,11 +101,21 @@ def tile_list_rod_batch_bench_kernel(
         def w1_piece(a, h):
             return w1[a * PASS : (a + 1) * PASS, h * PASS : (h + 1) * PASS]
 
-        def round_columns(grouped, raw, lo, hi):
+        def interleave_on_scalar(grouped, rows):
             nc.scalar.copy(
-                out=grouped[:, lo:hi, :].rearrange("p (c i) t -> p c t i", i=4),
-                in_=raw[:, :, lo:hi].rearrange("p t (c i) -> p c t i", i=4),
+                out=grouped.rearrange("p (c i) t -> p c t i", i=4),
+                in_=rows.rearrange("p t (c i) -> p c t i", i=4),
             )
+
+        def interleave_on_gpsimd(grouped, rows):
+            nc.gpsimd.tensor_scalar(
+                out=grouped, in0=rows.rearrange("p t c -> p c t"),
+                scalar1=1.0, scalar2=0.0, op0=ALU.mult, op1=ALU.add,
+            )
+
+        def round_columns(interleave, grouped, raw, lo, hi):
+            for first in range(lo, hi, P):
+                interleave(grouped[:, first : first + P, :], raw[:, :, first : first + P])
 
         def new_grouped():
             return stage.tile([P, PASS, PACK], BF16, name="grouped", tag="grouped", align_bytes=64)
@@ -105,16 +132,13 @@ def tile_list_rod_batch_bench_kernel(
 
         def early_weight(name, raw):
             grouped = new_grouped()
-            for lo in range(0, PASS, P):
-                round_columns(grouped, raw, lo, lo + P)
+            round_columns(interleave_on_scalar, grouped, raw, 0, PASS)
             return quantize_weight(name, grouped)
 
-        def pick_words(name, table, offsets):
+        def pick_words(name, table, list_tile):
             words = held(name, [P, S], U32)
             for lo, hi in ((0, CHUNK), (CHUNK, S)):
-                nc.vector.tensor_copy(
-                    words[:, lo:hi], table[:].indirect(offsets[:, lo // LIST_ROWS : hi // LIST_ROWS])
-                )
+                nc.vector.tensor_copy(words[:, lo:hi], table[:].indirect(entries(list_tile, lo, hi)))
             return words
 
         nc.sync.dma_start(rod_list[:], offs)
@@ -141,11 +165,11 @@ def tile_list_rod_batch_bench_kernel(
                     out=rod_plane[8 * a + 2 + e : P : 32, :].bitcast(I32),
                     in_=rod_scale_picked[16 + 8 * a + e : P : 32, :].bitcast(I32),
                 )
-        raw_10 = large.tile([P, PACK, PASS], F32, name="w1_raw_10", tag="large", align_bytes=64)
+        raw_10 = large_tile("w1_raw_10", [P, PACK, PASS], F32)
         for lo in (0, PASS // 2):
             nc.sync.dma_start(
                 out=raw_10[:, :, lo : lo + PASS // 2],
-                in_=w1_piece(1, 0)[:, lo : lo + PASS // 2].rearrange("(p t) c -> p t c", t=PACK),
+                in_=by_partition(w1_piece(1, 0)[:, lo : lo + PASS // 2]),
             )
         batch_plane = held("batch_plane", [P, S], U8)
         nc.vector.tensor_copy(batch_plane[:], batch_scale_table[:].indirect(batch_list[:]))
@@ -157,48 +181,54 @@ def tile_list_rod_batch_bench_kernel(
         gain_sb = held("gain_sb", [P, 2, PACK], F32)
         nc.sync.dma_start(out=gain_sb[:], in_=gain.rearrange("(h p t) -> p h t", h=2, t=PACK))
         nc.sync.dma_start(place_list[:], offs3)
-        picked = [pick_words("rod_words_0", rod_table_0, rod_list)]
+
+        rod_words = [pick_words("rod_words_0", rod_table_0, rod_list)]
         late_raw = [load_weight("w1_raw_01", w1_piece(0, 1))]
-        picked.append(pick_words("rod_words_1", rod_table_1, rod_list))
+        rod_words.append(pick_words("rod_words_1", rod_table_1, rod_list))
         late_raw.append(load_weight("w1_raw_11", w1_piece(1, 1)))
         late_raw.append(load_weight("w3_raw_0", w3[0:PASS, :]))
-        picked.append(pick_words("batch_words", batch_table, batch_list))
+        batch_words = pick_words("batch_words", batch_table, batch_list)
         late_raw.append(load_weight("w3_raw_1", w3[PASS : 2 * PASS, :]))
 
         z_codes = [held("z_codes_%d" % h, [P, S], U32) for h in range(2)]
         z_plane = [held("z_plane_%d" % h, [P, S], U8) for h in range(2)]
         late_grouped = []
-        late_mx = []
+        w3_mx = []
         pages = []
 
-        def late_weight_half(step):
-            piece, half = divmod(step, 2)
+        def round_late_half(piece, half):
             if half == 0:
                 late_grouped.append(new_grouped())
-            for lo in range(half * 2 * P, (half + 1) * 2 * P, P):
-                round_columns(late_grouped[piece], late_raw[piece], lo, lo + P)
+            interleave = interleave_on_gpsimd if piece < 2 and half == 1 else interleave_on_scalar
+            lo = half * PASS // 2
+            round_columns(interleave, late_grouped[piece], late_raw[piece], lo, lo + PASS // 2)
             if half == 1:
                 pages.append(load_page(piece))
+
+        units = [(2 * c + jj, h) for c, h in PRODUCT_ORDER for jj in range(2)]
+
+        def dealt(bank):
+            return bank[:].rearrange("j (m t) -> j t m", t=PACK)
 
         def first_products(step):
             jt, h = units[step]
             cols = slice(jt * P, (jt + 1) * P)
-            batch = banks[step % 2]
+            batch = banks[step % BATCH_BANKS]
             nc.tensor.matmul_mx(
                 out=batch[:],
-                lhsT=picked[2][:, cols].bitcast(FP8X4),
+                lhsT=batch_words[:, cols].bitcast(FP8X4),
                 lhsT_scale=batch_plane[:, cols],
                 rhs=w2_codes[:, 2 * h * PASS : 2 * (h + 1) * PASS].bitcast(FP4X4),
                 rhs_scale=w2_plane[:, h * PASS : (h + 1) * PASS],
                 start=True,
                 stop=True,
             )
-            rod = banks[2 + step % 3]
+            rod = banks[BATCH_BANKS + step % ROD_BANKS]
             for a in range(2):
                 codes, plane = w1_mx[a, h]
                 nc.tensor.matmul_mx(
                     out=rod[:],
-                    lhsT=picked[a][:, cols].bitcast(FP8X4),
+                    lhsT=rod_words[a][:, cols].bitcast(FP8X4),
                     lhsT_scale=rod_plane[8 * a : P, cols],
                     rhs=codes[:].bitcast(FP8X4),
                     rhs_scale=plane[:],
@@ -206,88 +236,70 @@ def tile_list_rod_batch_bench_kernel(
                     stop=(a == 1),
                 )
             batch_sb = work.tile([P, PACK, P], F32, name="batch_sb")
-            nc.scalar.copy(out=batch_sb[:], in_=batch[:].rearrange("j (m t) -> j t m", t=PACK))
+            nc.scalar.copy(out=batch_sb[:], in_=dealt(batch))
             return rod, batch_sb
 
         def combine(rod, batch_sb):
-            rod_dealt = rod[:].rearrange("j (m t) -> j t m", t=PACK)
-            larger = work.tile([P, PACK, P], F32, name="larger", bufs=16)
-            nc.vector.tensor_tensor(larger[:], rod_dealt, batch_sb[:], ALU.max)
-            product = work.tile([P, PACK, P], F32, name="product", bufs=16)
-            nc.vector.tensor_tensor(product[:], rod_dealt, batch_sb[:], ALU.mult)
+            larger = work.tile([P, PACK, P], F32, name="larger", bufs=len(units))
+            nc.vector.tensor_tensor(larger[:], dealt(rod), batch_sb[:], ALU.max)
+            product = work.tile([P, PACK, P], F32, name="product", bufs=len(units))
+            nc.vector.tensor_tensor(product[:], dealt(rod), batch_sb[:], ALU.mult)
             return larger, product
 
-        def gain_on_vector(c, h):
-            return c == 0 or (c, h) == (1, 0)
-
-        bent_tiles = {}
-
-        def bend(step, larger, product):
-            jt, h = units[step]
+        def transposed_sum(larger, product):
             summed = late_bank()[:].rearrange("p (t j) -> p t j", t=PACK)
             for t in range(PACK):
-                for term, first in ((larger, True), (product, False)):
+                for term, opens in ((larger, True), (product, False)):
                     nc.tensor.matmul(
                         summed[:, t, :], term[:, t, :], identity[:],
-                        start=first, stop=not first, is_transpose=True,
+                        start=opens, stop=not opens, is_transpose=True,
                     )
-            c, jj = divmod(jt, CHUNK // P)
-            if jj == 0:
-                bent_tiles[c, h] = stage.tile([P, PACK * CHUNK], F32, name="bent")
-            bent = bent_tiles[c, h]
-            if gain_on_vector(c, h):
+            return summed
+
+        def gain_on_vector(pair, h):
+            bent = stage.tile([P, CHUNK, PACK], F32, name="bent", tag="bent")
+            for jj in range(2):
+                summed = transposed_sum(*pair[jj])
                 nc.scalar.activation(
-                    bent[:].rearrange("p (j t) -> p j t", t=PACK)[:, jj * P : (jj + 1) * P, :],
-                    summed.rearrange("p t j -> p j t"),
-                    ACT.Tanh,
+                    bent[:, jj * P : (jj + 1) * P, :], summed.rearrange("p t j -> p j t"), ACT.Tanh
                 )
-            else:
+            z = stage.tile([P, CHUNK, PACK], BF16, name="z", tag="z", align_bytes=64)
+            spread = gain_sb[:, h, :].unsqueeze(1).to_broadcast([P, CHUNK, PACK])
+            nc.vector.tensor_tensor(z[:], bent[:], spread, ALU.mult)
+            return z
+
+        def gain_on_scalar(pair, h):
+            bent = stage.tile([P, PACK, CHUNK], F32, name="bent", tag="bent")
+            for jj in range(2):
+                summed = transposed_sum(*pair[jj])
+                nc.scalar.activation(bent[:, :, jj * P : (jj + 1) * P], summed, ACT.Tanh)
+            z = stage.tile([P, CHUNK, PACK], BF16, name="z", tag="z", align_bytes=64)
+            z_rows = stage.tile([P, PACK, CHUNK], BF16, name="z_rows")
+            for t in range(PACK):
                 nc.scalar.activation(
-                    bent[:].rearrange("p (t j) -> p t j", t=PACK)[:, :, jj * P : (jj + 1) * P],
-                    summed,
-                    ACT.Tanh,
+                    z_rows[:, t, :], bent[:, t, :], ACT.Copy, scale=gain_sb[:, h, t : t + 1]
                 )
+            interleave_on_scalar(z[:], z_rows[:])
+            return z
 
-        z_tiles = {}
-
-        def apply_gain(c, h):
-            bent = bent_tiles[c, h]
-            z = stage.tile([P, CHUNK, PACK], BF16, name="z", align_bytes=64)
-            if gain_on_vector(c, h):
-                nc.vector.tensor_tensor(
-                    z[:],
-                    bent[:].rearrange("p (j t) -> p j t", t=PACK),
-                    gain_sb[:, h, :].unsqueeze(1).to_broadcast([P, CHUNK, PACK]),
-                    ALU.mult,
-                )
-            else:
-                z_rows = stage.tile([P, PACK, CHUNK], BF16, name="z_rows")
-                for t in range(PACK):
-                    nc.scalar.activation(
-                        z_rows[:, t, :],
-                        bent[:, t * CHUNK : (t + 1) * CHUNK],
-                        ACT.Copy,
-                        scale=gain_sb[:, h, t : t + 1],
-                    )
-                nc.scalar.copy(
-                    out=z[:].rearrange("p (c i) t -> p c t i", i=4),
-                    in_=z_rows[:].rearrange("p t (c i) -> p c t i", i=4),
-                )
-            z_tiles[c, h] = z
-
-        def quantize_z(c, h):
+        def finish_part(index):
+            c, h = FINISH_ORDER[index]
+            first = units.index((2 * c, h))
+            apply_gain = gain_on_vector if index < VECTOR_GAIN_PARTS else gain_on_scalar
+            z = apply_gain(terms[first : first + 2], h)
             cols = slice(c * CHUNK, (c + 1) * CHUNK)
             nc.vector.quantize_mx(
                 out=z_codes[h][:, cols].bitcast(FP8X4),
                 scales=z_plane[h][:, cols],
-                in_=z_tiles[c, h][:].rearrange("p j t -> p (j t)"),
+                in_=z[:].rearrange("p j t -> p (j t)"),
             )
 
-        def place(lo, hi, i):
+        def place(c, i):
+            lo, hi = c * CHUNK, (c + 1) * CHUNK
             rows = slice(i * P, (i + 1) * P)
-            y = late_bank()[:, 0 : hi - lo]
+            y = late_bank()[:, 0:CHUNK]
             for h in range(2):
-                codes, plane = late_mx[2 + h]
+                codes, plane = w3_mx[h]
                 nc.tensor.matmul_mx(
                     out=y,
                     lhsT=codes[:, rows].bitcast(FP8X4),
@@ -297,48 +309,45 @@ def tile_list_rod_batch_bench_kernel(
                     start=(h == 0),
                     stop=(h == 1),
                 )
-            y_sb = work.tile([P, hi - lo], F32, name="y_sb", bufs=4)
+            y_sb = work.tile([P, CHUNK], F32, name="y_sb", bufs=ROW_TILES)
             nc.scalar.copy(out=y_sb[:], in_=y)
-            offsets = place_list[:, lo // LIST_ROWS : hi // LIST_ROWS]
-            nc.vector.tensor_tensor(pages[i][:].indirect(offsets), y_sb[:], wgo_sb[:, lo:hi], ALU.mult)
-            if hi == S:
+            window = pages[i][:].indirect(entries(place_list, lo, hi))
+            nc.vector.tensor_tensor(window, y_sb[:], wgo_sb[:, lo:hi], ALU.mult)
+            if c == CHUNKS - 1:
                 nc.sync.dma_start(out=out[rows, :], in_=pages[i][:])
 
-        def place_chunk(c, i):
-            place(c * CHUNK, (c + 1) * CHUNK, i)
-
-        def finish_half(c, h, placed):
-            first = units.index((2 * c, h))
-            for step in (first, first + 1):
-                bend(step, *terms[step])
-            apply_gain(c, h)
-            quantize_z(c, h)
-            for c_placed, i in placed:
-                place_chunk(c_placed, i)
-
-        order = [(0, 0), (1, 0), (2, 0), (0, 1), (1, 1), (3, 0), (2, 1), (3, 1)]
-        units = [(2 * c + jj, h) for c, h in order for jj in range(2)]
-        steps = 2 * TILES
-        halves = {2: (0, 0), 5: (1, 0), 8: (0, 1), 10: (1, 1), 12: (2, 0), 14: (2, 1), 15: (3, 0), 16: (3, 1)}
-        ready = [(c, i) for c in range(3) for i in range(4)]
-        terms = {}
-        sums = {0: first_products(0)}
-        for step in range(steps + 1):
-            if step + 1 < steps:
-                sums[step + 1] = first_products(step + 1)
-            if step < steps:
-                terms[step] = combine(*sums[step])
-            if step in (2, 4, 8, 10):
-                late_mx.append(quantize_weight("late_%d" % step, late_grouped[len(late_mx)]))
-            if len(late_mx) == 2:
-                w1_mx[0, 1], w1_mx[1, 1] = late_mx
-            if step == 8:
+        placings = [(c, i) for c in range(CHUNKS - 1) for i in range(ROW_TILES)]
+        first_placing = FINISH_ORDER.index((0, 1)) + 1
+        late_steps = list(range(4)) + list(range(W3_FIRST_STEP, W3_FIRST_STEP + 4))
+        late_halves = {step: divmod(n, 2) for n, step in enumerate(late_steps)}
+        finishes = {FIRST_FINISH_STEP + 2 * n: n for n in range(len(FINISH_ORDER))}
+        terms = []
+        sums = [first_products(0)]
+        for step in range(max(finishes) + 1):
+            if step + 1 < len(units):
+                sums.append(first_products(step + 1))
+            if step < len(units):
+                terms.append(combine(*sums[step]))
+            if step - 1 in late_halves and late_halves[step - 1][1] == 1:
+                piece = late_halves[step - 1][0]
+                quantized = quantize_weight("late_%d" % piece, late_grouped[piece])
+                if piece < 2:
+                    w1_mx[piece, 1] = quantized
+                else:
+                    w3_mx.append(quantized)
+            if step == W3_FIRST_STEP + 2:
                 wgo_sb = stage.tile([P, S], F32, name="wgo_sb", tag="grouped", align_bytes=64)
                 nc.sync.dma_start(out=wgo_sb[:], in_=wgo)
-            if step in (0, 1, 2, 3, 6, 7, 8, 9):
-                late_weight_half((0, 1, 2, 3, 6, 7, 8, 9).index(step))
-            if step in halves:
-                done = sorted(halves).index(step) - 3
-                finish_half(*halves[step], ready[2 * done : 2 * done + 2] if done >= 0 else [])
-        for c, i in ((2, 2), (3, 0), (3, 1), (3, 2), (2, 3), (3, 3)):
-            place_chunk(c, i)
+            if step in late_halves:
+                round_late_half(*late_halves[step])
+            if step in finishes:
+                finish_part(finishes[step])
+                done = finishes[step] - first_placing
+                for c, i in placings[2 * done : 2 * done + 2] if done >= 0 else []:
+                    place(c, i)
+        last = CHUNKS - 1
+        place(last - 1, ROW_TILES - 2)
+        for i in range(ROW_TILES - 1):
+            place(last, i)
+        place(last - 1, ROW_TILES - 1)
+        place(last, ROW_TILES - 1)

from contextlib import ExitStack

import concourse.mybir as mybir
from concourse.masks import make_identity

K, K2, H, N, T, S, T2 = 1024, 512, 1024, 512, 2048, 1024, 2048
FLOPS = 2 * (K * H * S + K2 * H * S + H * N * S)

F32 = mybir.dt.float32
BF16 = mybir.dt.bfloat16
I32 = mybir.dt.int32
U32 = mybir.dt.uint32
U16 = mybir.dt.uint16
U8 = mybir.dt.uint8
FP8X4 = mybir.dt.float8_e4m3fn_x4
FP4X4 = mybir.dt.float4_e2m1fn_x4
ALU = mybir.AluOpType
ACT = mybir.ActivationFunctionType

P = 128
PACK = 4
PASS = P * PACK
LIST_ROWS = 16
CHUNK = 2 * P
CHUNKS = S // CHUNK
ROW_TILES = N // P

PRODUCT_ORDER = [(0, 0), (1, 0), (2, 0), (0, 1), (1, 1), (3, 0), (2, 1), (3, 1)]
FINISH_ORDER = [(0, 0), (1, 0), (0, 1), (1, 1), (2, 0), (2, 1), (3, 0), (3, 1)]
FIRST_FINISH_STEP = 4
W3_FIRST_STEP = 6
VECTOR_GAIN_PARTS = 3
BATCH_BANKS, ROD_BANKS, LATE_BANKS = 2, 3, 3


def tile_list_rod_batch_bench_kernel(
    tc, tab_words, tab_scales, tab2_words, tab2_scales, offs, offs2, offs3,
    w1, w2_words, w2_scales, gain, w3, page1, wgo, out,
):
    nc = tc.nc
    with ExitStack() as ctx:
        keep = ctx.enter_context(tc.tile_pool(name="keep", bufs=1))
        stage = ctx.enter_context(tc.tile_pool(name="stage", bufs=2))
        work = ctx.enter_context(tc.tile_pool(name="work", bufs=3))
        large = ctx.enter_context(tc.tile_pool(name="large", bufs=ROW_TILES))
        psum = ctx.enter_context(tc.psum_pool(name="psum", bufs=1))

        def held(name, shape, dtype):
            return keep.tile(shape, dtype, name=name, align_bytes=64)

        def large_tile(name, shape, dtype):
            return large.tile(shape, dtype, name=name, tag="large", align_bytes=64)

        banks = [psum.tile([P, PASS], F32, name="bank_%d" % i) for i in range(8)]
        late_uses = []

        def late_bank():
            late_uses.append(banks[BATCH_BANKS + ROD_BANKS + len(late_uses) % LATE_BANKS])
            return late_uses[-1]

        rod_list = held("rod_list", [P, S // LIST_ROWS], U16)
        batch_list = held("batch_list", [P, S // LIST_ROWS], U16)
        place_list = held("place_list", [P, S // LIST_ROWS], U16)

        def entries(list_tile, lo, hi):
            return list_tile[:, lo // LIST_ROWS : hi // LIST_ROWS]

        rod_scale_table = held("rod_scale_table", [P, T], U8)
        batch_scale_table = held("batch_scale_table", [P, T], U8)
        w2_plane = held("w2_plane", [P, H], U8)
        for cleared in (rod_scale_table, batch_scale_table, w2_plane):
            nc.gpsimd.memset(cleared[:].bitcast(I32), 0)

        def by_partition(rows):
            return rows.rearrange("(p t) c -> p t c", t=PACK)

        def load_weight(name, rows):
            raw = large_tile(name, [P, PACK, PASS], F32)
            nc.sync.dma_start(out=raw[:], in_=by_partition(rows))
            return raw

        def load_table(name, words):
            table = large_tile(name, [P, T], U32)
            nc.sync.dma_start(
                out=table[:].bitcast(I32), in_=words.rearrange("p t i -> p (t i)").bitcast(I32)
            )
            return table

        def load_page(i):
            page = large_tile("page_%d" % i, [P, T2], F32)
            nc.sync.dma_start(out=page[:], in_=page1[i * P : (i + 1) * P, :])
            return page

        def load_scale_rows(queue, plane, rows):
            for d in range(4):
                queue.dma_start(
                    out=plane[32 * d : 32 * d + 4, :].bitcast(I32),
                    in_=rows[4 * d : 4 * d + 4, :].bitcast(I32),
                )

        def w1_piece(a, h):
            return w1[a * PASS : (a + 1) * PASS, h * PASS : (h + 1) * PASS]

        def interleave_on_scalar(grouped, rows):
            nc.scalar.copy(
                out=grouped.rearrange("p (c i) t -> p c t i", i=4),
                in_=rows.rearrange("p t (c i) -> p c t i", i=4),
            )

        def interleave_on_gpsimd(grouped, rows):
            nc.gpsimd.tensor_scalar(
                out=grouped, in0=rows.rearrange("p t c -> p c t"),
                scalar1=1.0, scalar2=0.0, op0=ALU.mult, op1=ALU.add,
            )

        def round_columns(interleave, grouped, raw, lo, hi):
            for first in range(lo, hi, P):
                interleave(grouped[:, first : first + P, :], raw[:, :, first : first + P])

        def new_grouped():
            return stage.tile([P, PASS, PACK], BF16, name="grouped", tag="grouped", align_bytes=64)

        def quantize_weight(name, grouped):
            codes = held(name + "_codes", [P, PASS], U32)
            plane = held(name + "_plane", [P, PASS], U8)
            nc.vector.quantize_mx(
                out=codes[:].bitcast(FP8X4),
                scales=plane[:],
                in_=grouped[:].rearrange("p c t -> p (c t)"),
            )
            return codes, plane

        def early_weight(name, raw):
            grouped = new_grouped()
            round_columns(interleave_on_scalar, grouped, raw, 0, PASS)
            return quantize_weight(name, grouped)

        def pick_words(name, table, list_tile):
            words = held(name, [P, S], U32)
            for lo, hi in ((0, CHUNK), (CHUNK, S)):
                nc.vector.tensor_copy(words[:, lo:hi], table[:].indirect(entries(list_tile, lo, hi)))
            return words

        nc.sync.dma_start(rod_list[:], offs)
        nc.sync.dma_start(batch_list[:], offs2)
        rod_rows = tab_scales.bitcast(I32).rearrange("a (g e) t -> e g a t", e=2)
        for e in range(2):
            nc.sync.dma_start(out=rod_scale_table[e:P:8, :].bitcast(I32), in_=rod_rows[e])
        raw_00 = load_weight("w1_raw_00", w1_piece(0, 0))
        load_scale_rows(nc.sync, batch_scale_table, tab2_scales[0])
        rod_table_0 = load_table("rod_table_0", tab_words[0])
        rod_table_1 = load_table("rod_table_1", tab_words[1])
        load_scale_rows(nc.gpsimd, w2_plane, w2_scales[0])

        identity = held("identity", [P, P], F32)
        make_identity(nc, identity[:])

        rod_scale_picked = held("rod_scale_picked", [P, S], U8)
        nc.vector.tensor_copy(rod_scale_picked[:], rod_scale_table[:].indirect(rod_list[:]))
        rod_plane = held("rod_plane", [P, S], U8)
        nc.vector.tensor_copy(rod_plane[:].bitcast(I32), rod_scale_picked[:].bitcast(I32))
        for a in range(2):
            for e in range(2):
                nc.sync.dma_start(
                    out=rod_plane[8 * a + 2 + e : P : 32, :].bitcast(I32),
                    in_=rod_scale_picked[16 + 8 * a + e : P : 32, :].bitcast(I32),
                )
        raw_10 = large_tile("w1_raw_10", [P, PACK, PASS], F32)
        for lo in (0, PASS // 2):
            nc.sync.dma_start(
                out=raw_10[:, :, lo : lo + PASS // 2],
                in_=by_partition(w1_piece(1, 0)[:, lo : lo + PASS // 2]),
            )
        batch_plane = held("batch_plane", [P, S], U8)
        nc.vector.tensor_copy(batch_plane[:], batch_scale_table[:].indirect(batch_list[:]))

        w1_mx = {(0, 0): early_weight("w1_00", raw_00), (1, 0): early_weight("w1_10", raw_10)}
        batch_table = load_table("batch_table", tab2_words[0])
        w2_codes = held("w2_codes", [P, 2 * H], U8)
        nc.sync.dma_start(out=w2_codes[:].bitcast(I32), in_=w2_words[0].bitcast(I32))
        gain_sb = held("gain_sb", [P, 2, PACK], F32)
        nc.sync.dma_start(out=gain_sb[:], in_=gain.rearrange("(h p t) -> p h t", h=2, t=PACK))
        nc.sync.dma_start(place_list[:], offs3)

        rod_words = [pick_words("rod_words_0", rod_table_0, rod_list)]
        late_raw = [load_weight("w1_raw_01", w1_piece(0, 1))]
        rod_words.append(pick_words("rod_words_1", rod_table_1, rod_list))
        late_raw.append(load_weight("w1_raw_11", w1_piece(1, 1)))
        late_raw.append(load_weight("w3_raw_0", w3[0:PASS, :]))
        batch_words = pick_words("batch_words", batch_table, batch_list)
        late_raw.append(load_weight("w3_raw_1", w3[PASS : 2 * PASS, :]))

        z_codes = [held("z_codes_%d" % h, [P, S], U32) for h in range(2)]
        z_plane = [held("z_plane_%d" % h, [P, S], U8) for h in range(2)]
        late_grouped = []
        w3_mx = []
        pages = []

        def round_late_half(piece, half):
            if half == 0:
                late_grouped.append(new_grouped())
            interleave = interleave_on_gpsimd if piece < 2 and half == 1 else interleave_on_scalar
            lo = half * PASS // 2
            round_columns(interleave, late_grouped[piece], late_raw[piece], lo, lo + PASS // 2)
            if half == 1:
                pages.append(load_page(piece))

        units = [(2 * c + jj, h) for c, h in PRODUCT_ORDER for jj in range(2)]

        def dealt(bank):
            return bank[:].rearrange("j (m t) -> j t m", t=PACK)

        def first_products(step):
            jt, h = units[step]
            cols = slice(jt * P, (jt + 1) * P)
            batch = banks[step % BATCH_BANKS]
            nc.tensor.matmul_mx(
                out=batch[:],
                lhsT=batch_words[:, cols].bitcast(FP8X4),
                lhsT_scale=batch_plane[:, cols],
                rhs=w2_codes[:, 2 * h * PASS : 2 * (h + 1) * PASS].bitcast(FP4X4),
                rhs_scale=w2_plane[:, h * PASS : (h + 1) * PASS],
                start=True,
                stop=True,
            )
            rod = banks[BATCH_BANKS + step % ROD_BANKS]
            for a in range(2):
                codes, plane = w1_mx[a, h]
                nc.tensor.matmul_mx(
                    out=rod[:],
                    lhsT=rod_words[a][:, cols].bitcast(FP8X4),
                    lhsT_scale=rod_plane[8 * a : P, cols],
                    rhs=codes[:].bitcast(FP8X4),
                    rhs_scale=plane[:],
                    start=(a == 0),
                    stop=(a == 1),
                )
            batch_sb = work.tile([P, PACK, P], F32, name="batch_sb")
            nc.scalar.copy(out=batch_sb[:], in_=dealt(batch))
            return rod, batch_sb

        def combine(rod, batch_sb):
            larger = work.tile([P, PACK, P], F32, name="larger", bufs=len(units))
            nc.vector.tensor_tensor(larger[:], dealt(rod), batch_sb[:], ALU.max)
            product = work.tile([P, PACK, P], F32, name="product", bufs=len(units))
            nc.vector.tensor_tensor(product[:], dealt(rod), batch_sb[:], ALU.mult)
            return larger, product

        def transposed_sum(larger, product):
            summed = late_bank()[:].rearrange("p (t j) -> p t j", t=PACK)
            for t in range(PACK):
                for term, opens in ((larger, True), (product, False)):
                    nc.tensor.matmul(
                        summed[:, t, :], term[:, t, :], identity[:],
                        start=opens, stop=not opens, is_transpose=True,
                    )
            return summed

        def gain_on_vector(pair, h):
            bent = stage.tile([P, CHUNK, PACK], F32, name="bent", tag="bent")
            for jj in range(2):
                summed = transposed_sum(*pair[jj])
                nc.scalar.activation(
                    bent[:, jj * P : (jj + 1) * P, :], summed.rearrange("p t j -> p j t"), ACT.Tanh
                )
            z = stage.tile([P, CHUNK, PACK], BF16, name="z", tag="z", align_bytes=64)
            spread = gain_sb[:, h, :].unsqueeze(1).to_broadcast([P, CHUNK, PACK])
            nc.vector.tensor_tensor(z[:], bent[:], spread, ALU.mult)
            return z

        def gain_on_scalar(pair, h):
            bent = stage.tile([P, PACK, CHUNK], F32, name="bent", tag="bent")
            for jj in range(2):
                summed = transposed_sum(*pair[jj])
                nc.scalar.activation(bent[:, :, jj * P : (jj + 1) * P], summed, ACT.Tanh)
            z = stage.tile([P, CHUNK, PACK], BF16, name="z", tag="z", align_bytes=64)
            z_rows = stage.tile([P, PACK, CHUNK], BF16, name="z_rows")
            for t in range(PACK):
                nc.scalar.activation(
                    z_rows[:, t, :], bent[:, t, :], ACT.Copy, scale=gain_sb[:, h, t : t + 1]
                )
            interleave_on_scalar(z[:], z_rows[:])
            return z

        def finish_part(index):
            c, h = FINISH_ORDER[index]
            first = units.index((2 * c, h))
            apply_gain = gain_on_vector if index < VECTOR_GAIN_PARTS else gain_on_scalar
            z = apply_gain(terms[first : first + 2], h)
            cols = slice(c * CHUNK, (c + 1) * CHUNK)
            nc.vector.quantize_mx(
                out=z_codes[h][:, cols].bitcast(FP8X4),
                scales=z_plane[h][:, cols],
                in_=z[:].rearrange("p j t -> p (j t)"),
            )

        def place(c, i):
            lo, hi = c * CHUNK, (c + 1) * CHUNK
            rows = slice(i * P, (i + 1) * P)
            y = late_bank()[:, 0:CHUNK]
            for h in range(2):
                codes, plane = w3_mx[h]
                nc.tensor.matmul_mx(
                    out=y,
                    lhsT=codes[:, rows].bitcast(FP8X4),
                    lhsT_scale=plane[:, rows],
                    rhs=z_codes[h][:, lo:hi].bitcast(FP8X4),
                    rhs_scale=z_plane[h][:, lo:hi],
                    start=(h == 0),
                    stop=(h == 1),
                )
            y_sb = work.tile([P, CHUNK], F32, name="y_sb", bufs=ROW_TILES)
            nc.scalar.copy(out=y_sb[:], in_=y)
            window = pages[i][:].indirect(entries(place_list, lo, hi))
            nc.vector.tensor_tensor(window, y_sb[:], wgo_sb[:, lo:hi], ALU.mult)
            if c == CHUNKS - 1:
                nc.sync.dma_start(out=out[rows, :], in_=pages[i][:])

        placings = [(c, i) for c in range(CHUNKS - 1) for i in range(ROW_TILES)]
        first_placing = FINISH_ORDER.index((0, 1)) + 1
        late_steps = list(range(4)) + list(range(W3_FIRST_STEP, W3_FIRST_STEP + 4))
        late_halves = {step: divmod(n, 2) for n, step in enumerate(late_steps)}
        finishes = {FIRST_FINISH_STEP + 2 * n: n for n in range(len(FINISH_ORDER))}
        terms = []
        sums = [first_products(0)]
        for step in range(max(finishes) + 1):
            if step + 1 < len(units):
                sums.append(first_products(step + 1))
            if step < len(units):
                terms.append(combine(*sums[step]))
            if step - 1 in late_halves and late_halves[step - 1][1] == 1:
                piece = late_halves[step - 1][0]
                quantized = quantize_weight("late_%d" % piece, late_grouped[piece])
                if piece < 2:
                    w1_mx[piece, 1] = quantized
                else:
                    w3_mx.append(quantized)
            if step == W3_FIRST_STEP + 2:
                wgo_sb = stage.tile([P, S], F32, name="wgo_sb", tag="grouped", align_bytes=64)
                nc.sync.dma_start(out=wgo_sb[:], in_=wgo)
            if step in late_halves:
                round_late_half(*late_halves[step])
            if step in finishes:
                finish_part(finishes[step])
                done = finishes[step] - first_placing
                for c, i in placings[2 * done : 2 * done + 2] if done >= 0 else []:
                    place(c, i)
        last = CHUNKS - 1
        place(last - 1, ROW_TILES - 2)
        for i in range(ROW_TILES - 1):
            place(last, i)
        place(last - 1, ROW_TILES - 1)
        place(last, ROW_TILES - 1)
